import numpy as np
import ml_dtypes


def mxq(x, axis, fmt="e4m3"):
    dtype, down = {"e4m3": (ml_dtypes.float8_e4m3fn, 7), "e5m2": (ml_dtypes.float8_e5m2, 14)}[fmt]
    v = np.moveaxis(np.asarray(x, np.float32).astype(ml_dtypes.bfloat16).astype(np.float64), axis, -1)
    blocks = v.reshape(v.shape[:-1] + (-1, 32))
    amax = np.abs(blocks).max(-1, keepdims=True)
    byte = np.maximum(np.where(amax > 0, np.frexp(amax)[1] - 1 + 127, 0) - down, 1)
    scale = np.exp2(byte - 127.0)
    codes = (blocks / scale).astype(np.float32).astype(dtype).astype(np.float64)
    return np.moveaxis((codes * scale).reshape(v.shape), -1, axis)


WIDE = False


def mx_kscale(k):
    if not WIDE:
        return np.ones(k)
    levels = np.array([10, -10, 5, -5, 0])
    if k % 512:
        return np.exp2(np.random.permutation(np.resize(levels, k // 32))).repeat(32)
    a = np.empty((k // 512, 16))
    for p in range(k // 512):
        a[p, :8] = np.random.permutation(np.resize(levels, 8))
        for g in range(8):
            far = levels[np.abs(levels - a[p, g]) >= 10]
            a[p, g + 8] = far[np.random.randint(len(far))]
    return np.exp2(a.ravel()).repeat(32)


BF16 = ml_dtypes.bfloat16


def bf(x):
    return np.asarray(x, np.float32).astype(BF16)


def f64(x):
    return np.asarray(x).astype(np.float64)


E2M1 = np.array([0.0, 0.5, 1.0, 1.5, 2.0, 3.0, 4.0, 6.0, -0.0, -0.5, -1.0, -1.5, -2.0, -3.0, -4.0, -6.0])


def pack_weight(w, fmt):
    k, n = w.shape
    w = f64(bf(w)).reshape(k // 32, 32, n)
    amax = np.abs(w).max(1)
    if fmt == "e4m3":
        byte = np.frexp(amax)[1] - 1 + 127 - 7
    else:
        mant, ex = np.frexp(amax / 6.0)
        byte = np.where(mant > 0.5, ex, ex - 1) + 127
    byte = np.clip(np.where(amax > 0, byte, 1), 1, 254)
    scaled = (w * np.exp2(127.0 - byte)[:, None, :]).reshape(k, n).astype(np.float32)
    by_word = np.ascontiguousarray(scaled.reshape(k // 512, 128, 4, n).transpose(0, 1, 3, 2))
    if fmt == "e4m3":
        words = by_word.astype(ml_dtypes.float8_e4m3fn).view(np.uint8)
    else:
        c = by_word.astype(ml_dtypes.float4_e2m1fn).view(np.uint8) & 0xF
        words = c[..., 0::2] | (c[..., 1::2] << 4)
    return np.ascontiguousarray(words), np.ascontiguousarray(byte.astype(np.uint8).reshape(k // 512, 16, n))


def unpack_weight(words, scales, fmt):
    g, p, n, _ = words.shape
    if fmt == "e4m3":
        vals = np.ascontiguousarray(words).view(ml_dtypes.float8_e4m3fn).astype(np.float64)
    else:
        nib = np.empty((g, p, n, 4), np.uint8)
        nib[..., 0::2] = words & 0xF
        nib[..., 1::2] = words >> 4
        vals = E2M1[nib]
    vals = vals * np.repeat(np.exp2(scales.astype(np.float64) - 127.0), 8, axis=1)[..., None]
    return vals.transpose(0, 1, 3, 2).reshape(g * 512, n)
def pack4(w):
    words, scales = pack_weight(w, "e2m1")
    return words.reshape(words.shape[0], 128, -1), scales


def unpack4(words, scales):
    return unpack_weight(words.reshape(words.shape[0], 128, -1, 2), scales, "e2m1")


def planes(Y):
    n, m = Y.shape
    b = f64(bf(Y)).reshape(n // 32, 32, m)
    amax = np.abs(b).max(1)
    byte = np.clip(np.where(amax > 0, np.frexp(amax)[1] - 1 + 127 - 7, 1), 1, 254)
    codes = (b * np.exp2(127.0 - byte)[:, None, :]).reshape(n, m).astype(np.float32).astype(ml_dtypes.float8_e4m3fn).view(np.uint8)
    words = codes.reshape(n // 512, 128, 4, m).transpose(0, 1, 3, 2)
    return np.ascontiguousarray(words), np.ascontiguousarray(byte.astype(np.uint8).reshape(n // 512, 16, m))


R, N, D, C, M, J = 1024, 1024, 1024, 512, 4, 7


def density_projection(h, w_words, w_scales, e):
    u = mxq(f64(h), 1, "e4m3") @ unpack4(w_words, w_scales)
    return mxq(f64(e), 2, "e4m3") @ mxq(u, 0, "e4m3")


def setup_inputs():
    s = mx_kscale(D)
    t = mx_kscale(N)
    h = np.random.standard_normal((N, D)) * s[None, :] * t[:, None]
    w = np.random.standard_normal((D, C)) / np.sqrt(D) / s[:, None]
    words, scales = pack4(w)
    e = np.random.standard_normal((M, R, N)) / np.sqrt(N) / t[None, None, :]
    coef = np.random.standard_normal((J, C)) * 0.4
    return {"h": bf(h), "w_words": words, "w_scales": scales, "e": bf(e), "coef": bf(coef)}


def core(h, w_words, w_scales, e, coef):
    am = density_projection(h, w_words, w_scales, e)
    coef = f64(coef)

    s = am[0]
    t = (am[1] ** 2 + am[2] ** 2 + am[3] ** 2) / 3.0

    b0 = (coef[0][None, :] * s
          + coef[1][None, :] * s ** 2
          + coef[2][None, :] * t
          + coef[3][None, :] * s * t)

    q = coef[4][None, :] + coef[5][None, :] * s + coef[6][None, :] * t
    b1 = am[1] * q
    b2 = am[2] * q
    b3 = am[3] * q

    return np.stack([b0, b1, b2, b3], axis=0)


def reference(h, w_words, w_scales, e, coef):
    R_out = core(h, w_words, w_scales, e, coef)
    words, scales = planes(np.moveaxis(R_out, 1, 0).reshape(1024, -1))
    return R_out, words, scales

@@ -1,0 +1,422 @@
+import math
+from contextlib import ExitStack
+
+import concourse.mybir as mybir
+from concourse.masks import make_identity
+
+F32 = mybir.dt.float32
+BF16 = mybir.dt.bfloat16
+I32 = mybir.dt.int32
+U32 = mybir.dt.uint32
+U8 = mybir.dt.uint8
+FP8X4 = mybir.dt.float8_e4m3fn_x4
+FP4X4 = mybir.dt.float4_e2m1fn_x4
+ACT = mybir.ActivationFunctionType
+ALU = mybir.AluOpType
+
+P = 128
+R, N, D, C, M, J = 1024, 1024, 1024, 512, 4, 7
+FLOPS = 2 * N * D * C + 2 * M * R * N * C
+UNITS = 16
+SORTED = ()
+VCOPY = (1, 3, 5, 7, 9, 11, 13, 15, 17)
+G_ENG = "gpsimd"
+M_ORDER = (2, 3, 1, 0)
+RAW_SLOTS, STAGE_SLOTS, CODE_SLOTS, OUT_SLOTS, OBF_SLOTS = 6, 3, 12, 4, 12
+
+
+def tile_macedensitytricksymmetriccontraction_x2_kernel(tc, h, w_words, w_scales, e, coef, out_0, out_1, out_2):
+    nc = tc.nc
+    with ExitStack() as ctx:
+        sb = ctx.enter_context(tc.tile_pool(name="sb", bufs=1))
+        ps = ctx.enter_context(tc.psum_pool(name="ps", bufs=1))
+        ctx.enter_context(tc.manual_schedule())
+
+        def ring(name, count, shape, dtype):
+            return [sb.tile(shape, dtype, name="%s%d" % (name, i), align_bytes=64) for i in range(count)]
+
+        banks = [ps.tile([P, 512], F32, name="bank%d" % i) for i in range(8)]
+        t_bank, back_bank = banks[4], banks[5]
+        ident = sb.tile([P, P], F32, name="ident", align_bytes=64)
+        coef_rows = sb.tile([P, C], BF16, name="coef_rows", align_bytes=64)
+        coef_f32 = sb.tile([P, C], F32, name="coef_f32", align_bytes=64)
+        coef_cols = sb.tile([P, 4, 8], F32, name="coef_cols", align_bytes=64)
+        w_codes = sb.tile([P, 2, 2 * C], U8, name="w_codes", align_bytes=64)
+        w_plane = sb.tile([P, 2, C], U8, name="w_plane", align_bytes=64)
+        raw = ring("raw", RAW_SLOTS, [P, 4, 1024], BF16)
+        sorted_words = ring("sorted_words", 4, [P, 512], F32)
+        stage = ring("stage", STAGE_SLOTS, [P, 2048], BF16)
+        codes = ring("codes", CODE_SLOTS, [P, 512], U32)
+        planes = ring("planes", CODE_SLOTS, [P, 512], U8)
+        u_stage = ring("u_stage", 2, [P, 2, 2, 512], BF16)
+        u_codes = ring("u_codes", 2, [P, 512], U32)
+        u_planes = ring("u_planes", 2, [P, 512], U8)
+        squares = ring("squares", 2, [P, 3, 256], F32)
+        affine = ring("affine", 2, [P, 2, 256], F32)
+        qp = ring("qp", 2, [P, 2, 256], F32)
+        b0_t = ring("b0_t", 2, [P, 256], F32)
+        q_rows = ring("q_rows", 2, [P, 256], F32)
+        o_f32 = ring("o_f32", OUT_SLOTS, [P, M, 4, 256], F32)
+        o_bf = sb.tile([P, OBF_SLOTS, 512], BF16, name="o_bf", align_bytes=64)
+        o_codes = ring("o_codes", 2, [P, M * C], U32)
+        o_planes = ring("o_planes", 2, [P, M * C], U8)
+
+        def unit(k):
+            if k < 12:
+                return [(k // 8, (k // 2) % 4, 2 * (k % 2) + jj) for jj in range(2)]
+            return [(1, t, k - 12) for t in (2, 3)]
+
+        def bank_pair(k):
+            first = 2 * (k % 2) if k < 12 else (6, 0, 2, 6)[k - 12]
+            return banks[first : first + 2]
+
+        def load(s, part):
+            if s < 2:
+                src = h[512 * s : 512 * (s + 1), :].rearrange("(p t) k -> p t k", t=4)[:, part, :]
+                nc.sync.dma_start(out=raw[s][:, part, :], in_=src)
+            else:
+                g, t = (s - 2) // 4, (s - 2) % 4
+                src = e[:, 512 * g : 512 * (g + 1), :].rearrange("m (p t) k -> p t m k", t=4)[:, t, part, :]
+                nc.sync.dma_start(out=raw[s % RAW_SLOTS][:, part, :], in_=src)
+
+        def sort_words(n):
+            if n in SORTED:
+                s, a = n // 4, n % 4
+                words = raw[s % RAW_SLOTS][:, a if s < 2 else M_ORDER[a], :].bitcast(F32)
+                nc.vector.tensor_copy(out=sorted_words[n % 4][:].rearrange("p (g u r) -> p g u r", g=2, u=2), in_=words.rearrange("p (g r u) -> p g u r", g=2, u=2))
+
+        def turn_in(n, bank, on_vector):
+            s, a = n // 4, n % 4
+            words = raw[s % RAW_SLOTS][:, a if s < 2 else M_ORDER[a], :].bitcast(F32)
+            for gk in range(2):
+                for u in range(2):
+                    col = (2 * gk + u) * P
+                    if n in SORTED:
+                        nc.tensor.transpose(bank[:, col : col + P], sorted_words[n % 4][:, col : col + P], ident[:])
+                    else:
+                        nc.tensor.transpose(bank[:, col : col + P], words[:, 256 * gk + u : 256 * (gk + 1) : 2], ident[:])
+            dst = stage[(n // 2) % STAGE_SLOTS][:, 1024 * (n % 2) : 1024 * (n % 2 + 1)].bitcast(F32).rearrange("p (g r u) -> p g r u", g=2, u=2)
+            src = bank[:].rearrange("p (g u r) -> p g r u", g=2, u=2)
+            if on_vector:
+                nc.vector.tensor_copy(out=dst, in_=src)
+            else:
+                nc.scalar.copy(out=dst, in_=src)
+
+        def quantise_in(i):
+            nc.vector.quantize_mx(out=codes[i % CODE_SLOTS][:].bitcast(FP8X4), scales=planes[i % CODE_SLOTS][:], in_=stage[i % STAGE_SLOTS][:])
+
+        def tile_operand(n, gk):
+            cols = slice(256 * (n % 2) + P * gk, 256 * (n % 2) + P * (gk + 1))
+            i = (n // 2) % CODE_SLOTS
+            return codes[i][:, cols].bitcast(FP8X4), planes[i][:, cols]
+
+        def mix(g, j, bank, on_vector):
+            for t in range(4):
+                for gk in range(2):
+                    h_codes, h_plane = tile_operand(4 * g + t, gk)
+                    nc.tensor.matmul_mx(
+                        out=bank[:, P * t : P * (t + 1)],
+                        lhsT=h_codes,
+                        lhsT_scale=h_plane,
+                        rhs=w_codes[:, gk, 256 * j : 256 * (j + 1)].bitcast(FP4X4),
+                        rhs_scale=w_plane[:, gk, P * j : P * (j + 1)],
+                        start=(gk == 0),
+                        stop=(gk == 1),
+                    )
+            dst = u_stage[j // 2][:, g, j % 2, :].rearrange("p (c t) -> p c t", t=4)
+            src = bank[:].rearrange("p (t c) -> p c t", t=4)
+            if on_vector:
+                nc.vector.tensor_copy(out=dst, in_=src)
+            else:
+                nc.scalar.copy(out=dst, in_=src)
+
+        def quantise_u(jp):
+            nc.vector.quantize_mx(out=u_codes[jp][:].bitcast(FP8X4), scales=u_planes[jp][:], in_=u_stage[jp][:].rearrange("p g j c -> p (g j c)"))
+
+        def cf(k, jj, row):
+            return coef_cols[:, unit(k)[jj][2], row : row + 1]
+
+        def u_operand(j, gk, width):
+            cols = slice(256 * gk + P * (j % 2), 256 * gk + P * (j % 2) + width)
+            return u_codes[j // 2][:, cols].bitcast(FP8X4), u_planes[j // 2][:, cols]
+
+        def contract(out, stationary, moving):
+            for gk in range(2):
+                (l_codes, l_plane), (r_codes, r_plane) = stationary(gk), moving(gk)
+                nc.tensor.matmul_mx(out=out, lhsT=l_codes, lhsT_scale=l_plane, rhs=r_codes, rhs_scale=r_plane, start=(gk == 0), stop=(gk == 1))
+
+        def project(k):
+            blocks = unit(k)
+            first = [8 + 4 * (4 * g + t) for g, t, j in blocks]
+            pair = bank_pair(k)
+            sq = squares[k % 2]
+            width = 256 if first[0] == first[1] else P
+            for a in range(3):
+                for jj in range(256 // width):
+                    col = 256 * (a % 2) + P * jj
+                    contract(pair[a // 2][:, col : col + width], lambda gk: tile_operand(first[jj] + a, gk), lambda gk: u_operand(blocks[jj][2], gk, width))
+                if a == 1:
+                    nc.scalar.activation(out=sq[:, 0:2, :].rearrange("p a c -> p (a c)"), in_=pair[0][:], func=ACT.Square, scale=math.sqrt(1.0 / 3.0))
+            for jj in range(2):
+                contract(pair[1][:, 256 + P * jj : 256 + P * (jj + 1)], lambda gk: u_operand(blocks[jj][2], gk, P), lambda gk: tile_operand(first[jj] + 3, gk))
+            nc.scalar.activation(out=sq[:, 2, :], in_=pair[1][:, 0:256], func=ACT.Square, scale=math.sqrt(1.0 / 3.0))
+
+        def affine_in_s(k):
+            for a, (slope, offset) in enumerate(((5, 4), (1, 0))):
+                for jj in range(2):
+                    s_cols = bank_pair(k)[1][:, 256 + P * jj : 256 + P * (jj + 1)]
+                    nc.scalar.activation(out=affine[k % 2][:, a, P * jj : P * (jj + 1)], in_=s_cols, func=ACT.Identity, scale=cf(k, jj, slope), bias=cf(k, jj, offset))
+
+        def sum_squares(k):
+            for jj in range(2):
+                for a in range(3):
+                    nc.tensor.matmul(
+                        out=t_bank[:, P * jj : P * (jj + 1)],
+                        lhsT=squares[k % 2][:, a, P * jj : P * (jj + 1)],
+                        rhs=ident[:],
+                        start=(a == 0),
+                        stop=(a == 2),
+                        is_transpose=True,
+                    )
+
+        def factors(k):
+            for a, row in enumerate((6, 3)):
+                for jj in range(2):
+                    cols = slice(P * jj, P * (jj + 1))
+                    nc.vector.scalar_tensor_tensor(out=qp[k % 2][:, a, cols], in0=t_bank[:, cols], scalar=cf(k, jj, row), in1=affine[k % 2][:, a, cols], op0=ALU.mult, op1=ALU.add)
+
+        def s_times_p(k):
+            nc.vector.tensor_tensor(out=b0_t[k % 2][:], in0=bank_pair(k)[1][:, 256:512], in1=qp[k % 2][:, 1, :], op=ALU.mult)
+
+        def finish_b0(k):
+            for jj in range(2):
+                cols = slice(P * jj, P * (jj + 1))
+                nc.vector.scalar_tensor_tensor(out=b0_t[k % 2][:, cols], in0=t_bank[:, cols], scalar=cf(k, jj, 2), in1=b0_t[k % 2][:, cols], op0=ALU.mult, op1=ALU.add)
+
+        def out_tile(k):
+            (g, t, j), (g_last, t_last, j_last) = unit(k)
+            o = o_f32[2 * g + j // 2]
+            if t == t_last:
+                return o[:, :, t, :].rearrange("p m (b c) -> p m b c", b=2)
+            return o[:, :, t : t + 2, P * (j % 2) : P * (j % 2 + 1)]
+
+        def turn_back(side, src):
+            for jj in range(2):
+                col = 256 * side + P * jj
+                nc.tensor.transpose(back_bank[:, col : col + P], src[:, P * jj : P * (jj + 1)], ident[:])
+
+        def copy_q(k):
+            nc.scalar.copy(out=q_rows[k % 2][:], in_=back_bank[:, 0:256])
+
+        def copy_b0(k):
+            nc.scalar.copy(out=out_tile(k)[:, 0, :, :], in_=back_bank[:, 256:512].rearrange("p (b c) -> p b c", b=2))
+
+        def products(k, half):
+            bank, o, q = bank_pair(k)[half], out_tile(k), q_rows[k % 2]
+            if half == 0:
+                nc.vector.tensor_tensor(
+                    out=o[:, 2:4, :, :],
+                    in0=bank[:].rearrange("p (a b c) -> p a b c", a=2, b=2),
+                    in1=q[:].rearrange("p (a b c) -> p a b c", a=1, b=2).to_broadcast([P, 2, 2, P]),
+                    op=ALU.mult,
+                )
+            else:
+                nc.vector.tensor_tensor(out=o[:, 1, :, :], in0=bank[:, 0:256].rearrange("p (b c) -> p b c", b=2), in1=q[:].rearrange("p (b c) -> p b c", b=2), op=ALU.mult)
+
+        def store_rows(k):
+            (g, t, j), (g_last, t_last, j_last) = unit(k)
+            rows = out_0[:, 512 * g : 512 * (g + 1), P * j : P * (j_last + 1)].rearrange("m (p t) c -> p m t c", t=4)
+            for tt in range(t, t_last + 1):
+                nc.sync.dma_start(out=rows[:, :, tt, :], in_=o_f32[2 * g + j // 2][:, :, tt, P * (j % 2) : P * (j_last % 2 + 1)])
+
+        def round_out(n, count, slot, eng):
+            g, j, m = n // 16, (n // 4) % 4, (n + 2) % 4
+            dst = o_bf[:, slot : slot + count, :].rearrange("p m (c t) -> p m c t", t=4)
+            src = o_f32[2 * g + j // 2][:, m : m + count, :, P * (j % 2) : P * (j % 2 + 1)].rearrange("p m t c -> p m c t")
+            if eng == "vector":
+                nc.vector.tensor_copy(out=dst, in_=src)
+            elif eng == "scalar":
+                nc.scalar.copy(out=dst, in_=src)
+            else:
+                nc.gpsimd.tensor_scalar(out=dst, in0=src, scalar1=1.0, scalar2=0.0, op0=ALU.mult, op1=ALU.add)
+
+        def quantise_out(n, slot):
+            g, j, m = n // 16, (n // 4) % 4, (n + 2) % 4
+            cols = slice(C * m + P * j, C * m + P * (j + 1))
+            nc.vector.quantize_mx(out=o_codes[g][:, cols].bitcast(FP8X4), scales=o_planes[g][:, cols], in_=o_bf[:, slot, :])
+
+        def store_words(g, first, last):
+            dst = out_1[g].rearrange("p n t -> p (n t)").bitcast(I32).rearrange("p (m c) -> p m c", m=M)
+            src = o_codes[g][:].bitcast(I32).rearrange("p (m c) -> p m c", m=M)
+            nc.sync.dma_start(out=dst[:, :, P * first : P * last], in_=src[:, :, P * first : P * last])
+
+        def store_scales(g):
+            for quad in range(4):
+                nc.sync.dma_start(out=out_2[g, 4 * quad : 4 * quad + 4, :].bitcast(I32), in_=o_planes[g][32 * quad : 32 * quad + 4, :].bitcast(I32))
+
+        nc.scalar.dma_start(out=coef_rows[0:J, :], in_=coef)
+        nc.vector.memset(w_plane[:].rearrange("p g c -> p (g c)").bitcast(I32), 0)
+        make_identity(nc, ident[:])
+        nc.gpsimd.memset(coef_f32[:], 0.0)
+        load(0, slice(0, 1))
+        load(0, slice(1, 2))
+        load(0, slice(2, 4))
+        for quad in range(4):
+            nc.scalar.dma_start(
+                out=w_plane[32 * quad : 32 * quad + 4, :, :].bitcast(I32),
+                in_=w_scales[:, 4 * quad : 4 * quad + 4, :].rearrange("g r c -> r g c").bitcast(I32),
+            )
+        load(1, slice(0, 2))
+        load(1, slice(2, 4))
+        nc.sync.dma_start(out=w_codes[:].bitcast(I32), in_=w_words.rearrange("g p n -> p g n").bitcast(I32))
+        load(2, slice(2, 4))
+        load(2, slice(0, 2))
+        for s in range(3, RAW_SLOTS):
+            load(s, slice(0, 4))
+        nc.scalar.activation(out=coef_f32[0:J, :], in_=coef_rows[0:J, :], func=ACT.Identity)
+
+        for n in range(8):
+            sort_words(n + 2)
+            turn_in(n, banks[4 + n % 4], n in VCOPY)
+            if n % 2 == 0 and n > 1:
+                quantise_in(n // 2 - 1)
+            if n % 4 == 3:
+                load(RAW_SLOTS + n // 4, slice(0, 4))
+        mix(0, 0, banks[0], False)
+        quantise_in(3)
+        sort_words(10)
+        sort_words(11)
+        mix(0, 1, banks[1], False)
+        turn_in(8, banks[4], 8 in VCOPY)
+        turn_in(9, banks[5], 9 in VCOPY)
+        mix(1, 0, banks[2], False)
+        mix(1, 1, banks[3], False)
+        sort_words(12)
+        sort_words(13)
+        quantise_in(4)
+        turn_in(10, banks[6], 10 in VCOPY)
+        turn_in(11, banks[7], 11 in VCOPY)
+        load(RAW_SLOTS + 2, slice(0, 4))
+        quantise_u(0)
+        for j in range(4):
+            nc.tensor.transpose(banks[4][:, P * j : P * (j + 1)], coef_f32[:, P * j : P * (j + 1)], ident[:])
+        nc.vector.tensor_copy(out=coef_cols[:], in_=banks[4][:].rearrange("p (j r) -> p j r", j=4)[:, :, 0:8])
+        mix(0, 2, banks[5], False)
+        quantise_in(5)
+        mix(0, 3, banks[2], False)
+        sort_words(14)
+        sort_words(15)
+        turn_in(12, banks[6], 12 in VCOPY)
+        turn_in(13, banks[7], 13 in VCOPY)
+        mix(1, 2, banks[3], False)
+        mix(1, 3, banks[4], True)
+        project(0)
+        sort_words(16)
+        sort_words(17)
+        quantise_u(1)
+        quantise_in(6)
+        turn_in(14, banks[5], 14 in VCOPY)
+        turn_in(15, banks[6], 15 in VCOPY)
+        load(RAW_SLOTS + 3, slice(0, 4))
+        turn_in(16, banks[7], 16 in VCOPY)
+        turn_in(17, banks[5], 17 in VCOPY)
+        quantise_in(7)
+
+        plan = {
+            8: [(0, 2, "g")],
+            9: [(2, 2, "g"), (4, 1, "vector")],
+            10: [(6, 2, "g"), (5, 1, "vector")],
+            11: [(8, 2, "g"), (10, 2, "scalar")],
+            12: [(12, 2, "g"), (14, 2, "scalar")],
+            13: [(16, 2, "g"), (19, 1, "vector")],
+            14: [(20, 2, "g"), (23, 1, "vector"), (18, 1, "scalar")],
+            15: [(24, 2, "g"), (27, 1, "vector"), (22, 1, "scalar")],
+        }
+        base = {"g": 0, "vector": 4, "scalar": 6}
+
+        def slot_of(k, eng):
+            return base[eng] + (0 if eng == "g" else 4 * (k % 2))
+
+        def later_quantise(k):
+            return [lambda n=n + i, slot=slot_of(k, eng) + i: quantise_out(n, slot) for n, count, eng in plan.get(k, []) if eng != "g" for i in range(count)]
+
+        for k in range(UNITS):
+            tiles = [18 + 2 * k, 19 + 2 * k] if k <= 10 else []
+            mine = plan.get(k, [])
+            fill = later_quantise(k - 1)
+            if k == 0:
+                fill.append(lambda: quantise_in(8))
+            if tiles:
+                fill.append(lambda: quantise_in(tiles[0] // 2))
+            if k >= 1:
+                project(k)
+                turn_back(0, qp[(k - 1) % 2][:, 0, :])
+            if k >= 2:
+                turn_back(1, b0_t[k % 2][:])
+            if k >= 1:
+                copy_q(k - 1)
+                products(k - 1, 0)
+            affine_in_s(k)
+            if k >= 2:
+                copy_b0(k - 2)
+                store_rows(k - 2)
+            if k == 12:
+                store_words(0, 0, 2)
+            if k == 14:
+                store_words(0, 2, 4)
+                store_scales(0)
+            for n, count, eng in mine:
+                if eng == "g" and G_ENG == "gpsimd":
+                    round_out(n, count, 0, G_ENG)
+            if tiles:
+                turn_in(tiles[0], banks[6 + k % 2], False)
+            sum_squares(k)
+            factors(k)
+            if k >= 1:
+                products(k - 1, 1)
+            s_times_p(k)
+            if tiles:
+                turn_in(tiles[1], banks[7 - k % 2], False)
+            split = 1 if k < 13 else 0
+            for step in fill[0:split]:
+                step()
+            finish_b0(k)
+            for n, count, eng in mine:
+                if eng != "g":
+                    round_out(n, count, slot_of(k, eng), eng)
+                elif G_ENG != "gpsimd":
+                    round_out(n, count, 0, G_ENG)
+            for n in tiles:
+                sort_words(n + 2)
+            for step in fill[split:]:
+                step()
+            for n, count, eng in mine:
+                if eng == "g":
+                    for i in range(count):
+                        quantise_out(n + i, i)
+
+        last = UNITS - 1
+        turn_back(0, qp[last % 2][:, 0, :])
+        turn_back(1, b0_t[(last - 1) % 2][:])
+        copy_q(last)
+        copy_b0(last - 1)
+        store_rows(last - 1)
+        store_words(1, 0, 1)
+        turn_back(1, b0_t[last % 2][:])
+        products(last, 0)
+        products(last, 1)
+        copy_b0(last)
+        store_rows(last)
+        round_out(28, 1, 4, "scalar")
+        round_out(26, 1, 6, "vector")
+        for step in later_quantise(last):
+            step()
+        round_out(29, 1, 5, "vector")
+        quantise_out(26, 6)
+        store_words(1, 1, 3)
+        round_out(30, 1, 2, "scalar")
+        round_out(31, 1, 3, "vector")
+        for n, slot in ((29, 5), (28, 4), (31, 3), (30, 2)):
+            quantise_out(n, slot)
+        store_scales(1)
+        store_words(1, 3, 4)

@@ -18,8 +18,8 @@ P = 128
 R, N, D, C, M, J = 1024, 1024, 1024, 512, 4, 7
 FLOPS = 2 * N * D * C + 2 * M * R * N * C
 UNITS = 16
-SORTED = ()
-VCOPY = (1, 3, 5, 7, 9, 11, 13, 15, 17)
+SORTED = range(0, 20)
+VCOPY = ()
 G_ENG = "gpsimd"
 M_ORDER = (2, 3, 1, 0)
 RAW_SLOTS, STAGE_SLOTS, CODE_SLOTS, OUT_SLOTS, OBF_SLOTS = 6, 3, 12, 4, 12
@@ -180,7 +180,7 @@ def tile_macedensitytricksymmetriccontraction_x2_kernel(tc, h, w_words, w_scales
                     )
 
         def factors(k):
-            for a, row in enumerate((6, 3)):
+            for a, row in ((1, 3), (0, 6)):
                 for jj in range(2):
                     cols = slice(P * jj, P * (jj + 1))
                     nc.vector.scalar_tensor_tensor(out=qp[k % 2][:, a, cols], in0=t_bank[:, cols], scalar=cf(k, jj, row), in1=affine[k % 2][:, a, cols], op0=ALU.mult, op1=ALU.add)
@@ -223,11 +223,15 @@ def tile_macedensitytricksymmetriccontraction_x2_kernel(tc, h, w_words, w_scales
             else:
                 nc.vector.tensor_tensor(out=o[:, 1, :, :], in0=bank[:, 0:256].rearrange("p (b c) -> p b c", b=2), in1=q[:].rearrange("p (b c) -> p b c", b=2), op=ALU.mult)
 
-        def store_rows(k):
+        def store_rows(k, m_first, m_last):
             (g, t, j), (g_last, t_last, j_last) = unit(k)
             rows = out_0[:, 512 * g : 512 * (g + 1), P * j : P * (j_last + 1)].rearrange("m (p t) c -> p m t c", t=4)
-            for tt in range(t, t_last + 1):
-                nc.sync.dma_start(out=rows[:, :, tt, :], in_=o_f32[2 * g + j // 2][:, :, tt, P * (j % 2) : P * (j_last % 2 + 1)])
+            o = o_f32[2 * g + j // 2][:, :, :, P * (j % 2) : P * (j_last % 2 + 1)]
+            if m_last - m_first == 1:
+                nc.sync.dma_start(out=rows[:, m_first, t : t_last + 1, :], in_=o[:, m_first, t : t_last + 1, :])
+            else:
+                for tt in range(t, t_last + 1):
+                    nc.sync.dma_start(out=rows[:, m_first:m_last, tt, :], in_=o[:, m_first:m_last, tt, :])
 
         def round_out(n, count, slot, eng):
             g, j, m = n // 16, (n // 4) % 4, (n + 2) % 4
@@ -252,7 +256,7 @@ def tile_macedensitytricksymmetriccontraction_x2_kernel(tc, h, w_words, w_scales
 
         def store_scales(g):
             for quad in range(4):
-                nc.sync.dma_start(out=out_2[g, 4 * quad : 4 * quad + 4, :].bitcast(I32), in_=o_planes[g][32 * quad : 32 * quad + 4, :].bitcast(I32))
+                (nc.scalar if g == 1 and quad % 2 else nc.sync).dma_start(out=out_2[g, 4 * quad : 4 * quad + 4, :].bitcast(I32), in_=o_planes[g][32 * quad : 32 * quad + 4, :].bitcast(I32))
 
         nc.scalar.dma_start(out=coef_rows[0:J, :], in_=coef)
         nc.vector.memset(w_plane[:].rearrange("p g c -> p (g c)").bitcast(I32), 0)
@@ -267,156 +271,163 @@ def tile_macedensitytricksymmetriccontraction_x2_kernel(tc, h, w_words, w_scales
                 in_=w_scales[:, 4 * quad : 4 * quad + 4, :].rearrange("g r c -> r g c").bitcast(I32),
             )
         load(1, slice(0, 2))
-        load(1, slice(2, 4))
         nc.sync.dma_start(out=w_codes[:].bitcast(I32), in_=w_words.rearrange("g p n -> p g n").bitcast(I32))
+        load(1, slice(2, 4))
         load(2, slice(2, 4))
         load(2, slice(0, 2))
         for s in range(3, RAW_SLOTS):
             load(s, slice(0, 4))
         nc.scalar.activation(out=coef_f32[0:J, :], in_=coef_rows[0:J, :], func=ACT.Identity)
 
-        for n in range(8):
+        sort_words(0)
+        sort_words(1)
+        for n in range(6):
             sort_words(n + 2)
             turn_in(n, banks[4 + n % 4], n in VCOPY)
-            if n % 2 == 0 and n > 1:
+            if n in (2, 4):
                 quantise_in(n // 2 - 1)
-            if n % 4 == 3:
-                load(RAW_SLOTS + n // 4, slice(0, 4))
+            if n == 3:
+                load(RAW_SLOTS, slice(0, 4))
         mix(0, 0, banks[0], False)
-        quantise_in(3)
-        sort_words(10)
-        sort_words(11)
         mix(0, 1, banks[1], False)
+        quantise_in(2)
+        turn_in(6, banks[6], 6 in VCOPY)
+        turn_in(7, banks[7], 7 in VCOPY)
+        load(RAW_SLOTS + 1, slice(0, 4))
+        sort_words(8)
+        sort_words(9)
+        mix(0, 2, banks[2], False)
+        quantise_in(3)
+        mix(0, 3, banks[3], True)
         turn_in(8, banks[4], 8 in VCOPY)
         turn_in(9, banks[5], 9 in VCOPY)
-        mix(1, 0, banks[2], False)
-        mix(1, 1, banks[3], False)
-        sort_words(12)
-        sort_words(13)
+        sort_words(10)
+        sort_words(11)
+        mix(1, 0, banks[6], False)
+        mix(1, 1, banks[7], False)
         quantise_in(4)
-        turn_in(10, banks[6], 10 in VCOPY)
-        turn_in(11, banks[7], 11 in VCOPY)
+        turn_in(10, banks[0], 10 in VCOPY)
+        turn_in(11, banks[1], 11 in VCOPY)
         load(RAW_SLOTS + 2, slice(0, 4))
         quantise_u(0)
         for j in range(4):
             nc.tensor.transpose(banks[4][:, P * j : P * (j + 1)], coef_f32[:, P * j : P * (j + 1)], ident[:])
         nc.vector.tensor_copy(out=coef_cols[:], in_=banks[4][:].rearrange("p (j r) -> p j r", j=4)[:, :, 0:8])
-        mix(0, 2, banks[5], False)
+        sort_words(12)
+        sort_words(13)
+        mix(1, 2, banks[2], False)
         quantise_in(5)
-        mix(0, 3, banks[2], False)
         sort_words(14)
         sort_words(15)
-        turn_in(12, banks[6], 12 in VCOPY)
-        turn_in(13, banks[7], 13 in VCOPY)
-        mix(1, 2, banks[3], False)
-        mix(1, 3, banks[4], True)
+        mix(1, 3, banks[3], False)
+        turn_in(12, banks[5], 12 in VCOPY)
+        turn_in(13, banks[6], 13 in VCOPY)
         project(0)
+        quantise_u(1)
         sort_words(16)
         sort_words(17)
-        quantise_u(1)
-        quantise_in(6)
-        turn_in(14, banks[5], 14 in VCOPY)
-        turn_in(15, banks[6], 15 in VCOPY)
+        turn_in(14, banks[7], 14 in VCOPY)
+        turn_in(15, banks[5], 15 in VCOPY)
         load(RAW_SLOTS + 3, slice(0, 4))
-        turn_in(16, banks[7], 16 in VCOPY)
-        turn_in(17, banks[5], 17 in VCOPY)
+        quantise_in(6)
+        sort_words(18)
+        sort_words(19)
+        affine_in_s(0)
+        turn_in(16, banks[6], 16 in VCOPY)
+        sum_squares(0)
         quantise_in(7)
+        factors(0)
+        s_times_p(0)
+        turn_in(17, banks[7], 17 in VCOPY)
+        turn_in(18, banks[5], 18 in VCOPY)
+        turn_in(19, banks[6], 19 in VCOPY)
+        sort_words(20)
+        finish_b0(0)
+        quantise_in(8)
+        quantise_in(9)
 
         plan = {
-            8: [(0, 2, "g")],
-            9: [(2, 2, "g"), (4, 1, "vector")],
-            10: [(6, 2, "g"), (5, 1, "vector")],
-            11: [(8, 2, "g"), (10, 2, "scalar")],
-            12: [(12, 2, "g"), (14, 2, "scalar")],
-            13: [(16, 2, "g"), (19, 1, "vector")],
-            14: [(20, 2, "g"), (23, 1, "vector"), (18, 1, "scalar")],
-            15: [(24, 2, "g"), (27, 1, "vector"), (22, 1, "scalar")],
+            7: [(0, 2, "g", 0)],
+            8: [(4, 2, "g", 0)],
+            9: [(2, 2, "g", 0)],
+            10: [(6, 2, "g", 0)],
+            11: [(10, 1, "scalar", 10), (11, 1, "vector", 8), (8, 2, "g", 0)],
+            12: [(12, 2, "g", 0)],
+            13: [(16, 1, "scalar", 6), (17, 1, "vector", 4), (14, 2, "g", 0)],
+            14: [(20, 1, "scalar", 10), (21, 1, "vector", 8), (18, 2, "g", 0)],
+            15: [(24, 1, "scalar", 6), (25, 1, "vector", 4), (22, 2, "g", 0)],
         }
-        base = {"g": 0, "vector": 4, "scalar": 6}
 
-        def slot_of(k, eng):
-            return base[eng] + (0 if eng == "g" else 4 * (k % 2))
-
-        def later_quantise(k):
-            return [lambda n=n + i, slot=slot_of(k, eng) + i: quantise_out(n, slot) for n, count, eng in plan.get(k, []) if eng != "g" for i in range(count)]
-
-        for k in range(UNITS):
+        for k in range(1, UNITS):
             tiles = [18 + 2 * k, 19 + 2 * k] if k <= 10 else []
             mine = plan.get(k, [])
-            fill = later_quantise(k - 1)
-            if k == 0:
-                fill.append(lambda: quantise_in(8))
-            if tiles:
-                fill.append(lambda: quantise_in(tiles[0] // 2))
-            if k >= 1:
-                project(k)
-                turn_back(0, qp[(k - 1) % 2][:, 0, :])
-            if k >= 2:
-                turn_back(1, b0_t[k % 2][:])
-            if k >= 1:
-                copy_q(k - 1)
-                products(k - 1, 0)
+            project(k)
+            turn_back(0, qp[(k - 1) % 2][:, 0, :])
+            copy_q(k - 1)
+            products(k - 1, 0)
+            if k < 12:
+                products(k - 1, 1)
             affine_in_s(k)
-            if k >= 2:
-                copy_b0(k - 2)
-                store_rows(k - 2)
-            if k == 12:
+            for n, count, eng, slot in mine:
+                if eng == "g":
+                    round_out(n, count, slot, G_ENG)
+            if tiles:
+                turn_in(tiles[0], banks[7 - k % 2], False)
+            sum_squares(k)
+            turn_back(1, b0_t[(k - 1) % 2][:])
+            copy_b0(k - 1)
+            factors(k)
+            s_times_p(k)
+            if k >= 12:
+                products(k - 1, 1)
+            store_rows(k - 1, 0, 4)
+            if tiles:
+                turn_in(tiles[1], banks[6 + k % 2], tiles[1] in VCOPY)
+                sort_words(tiles[0] + 2)
+            finish_b0(k)
+            if tiles:
+                sort_words(tiles[1] + 2)
+            for n, count, eng, slot in mine:
+                if eng != "g":
+                    round_out(n, count, slot, eng)
+            if tiles:
+                quantise_in(tiles[0] // 2)
+            if k == UNITS - 1:
+                break
+            for n, count, eng, slot in mine:
+                for i in range(count):
+                    quantise_out(n + i, slot + i)
+            if k == 10:
                 store_words(0, 0, 2)
-            if k == 14:
+            if k == 13:
                 store_words(0, 2, 4)
                 store_scales(0)
-            for n, count, eng in mine:
-                if eng == "g" and G_ENG == "gpsimd":
-                    round_out(n, count, 0, G_ENG)
-            if tiles:
-                turn_in(tiles[0], banks[6 + k % 2], False)
-            sum_squares(k)
-            factors(k)
-            if k >= 1:
-                products(k - 1, 1)
-            s_times_p(k)
-            if tiles:
-                turn_in(tiles[1], banks[7 - k % 2], False)
-            split = 1 if k < 13 else 0
-            for step in fill[0:split]:
-                step()
-            finish_b0(k)
-            for n, count, eng in mine:
-                if eng != "g":
-                    round_out(n, count, slot_of(k, eng), eng)
-                elif G_ENG != "gpsimd":
-                    round_out(n, count, 0, G_ENG)
-            for n in tiles:
-                sort_words(n + 2)
-            for step in fill[split:]:
-                step()
-            for n, count, eng in mine:
-                if eng == "g":
-                    for i in range(count):
-                        quantise_out(n + i, i)
+            if k >= 14:
+                store_words(1, k - 14, k - 13)
 
         last = UNITS - 1
         turn_back(0, qp[last % 2][:, 0, :])
-        turn_back(1, b0_t[(last - 1) % 2][:])
         copy_q(last)
-        copy_b0(last - 1)
-        store_rows(last - 1)
-        store_words(1, 0, 1)
         turn_back(1, b0_t[last % 2][:])
+        round_out(26, 1, 2, "scalar")
         products(last, 0)
         products(last, 1)
+        store_rows(last, 1, 4)
         copy_b0(last)
-        store_rows(last)
-        round_out(28, 1, 4, "scalar")
-        round_out(26, 1, 6, "vector")
-        for step in later_quantise(last):
-            step()
-        round_out(29, 1, 5, "vector")
-        quantise_out(26, 6)
-        store_words(1, 1, 3)
-        round_out(30, 1, 2, "scalar")
-        round_out(31, 1, 3, "vector")
-        for n, slot in ((29, 5), (28, 4), (31, 3), (30, 2)):
+        store_rows(last, 0, 1)
+        round_out(27, 1, 3, "scalar")
+        round_out(28, 1, 8, "scalar")
+        round_out(30, 1, 10, "scalar")
+        for n, count, eng, slot in plan[last]:
+            for i in range(count):
+                quantise_out(n + i, slot + i)
+        store_words(1, 1, 2)
+        round_out(29, 1, 9, "vector")
+        round_out(31, 1, 11, "vector")
+        quantise_out(26, 2)
+        quantise_out(27, 3)
+        store_words(1, 2, 3)
+        for n, slot in ((29, 9), (31, 11), (28, 8), (30, 10)):
             quantise_out(n, slot)
-        store_scales(1)
         store_words(1, 3, 4)
+        store_scales(1)

@@ -18,8 +18,8 @@ P = 128
 R, N, D, C, M, J = 1024, 1024, 1024, 512, 4, 7
 FLOPS = 2 * N * D * C + 2 * M * R * N * C
 UNITS = 16
-SORTED = range(0, 20)
-VCOPY = ()
+SORTED = ()
+VCOPY = (1, 3, 7, 11, 15, 19, 21, 23, 25, 27, 29, 31, 33, 37)
 G_ENG = "gpsimd"
 M_ORDER = (2, 3, 1, 0)
 RAW_SLOTS, STAGE_SLOTS, CODE_SLOTS, OUT_SLOTS, OBF_SLOTS = 6, 3, 12, 4, 12
@@ -38,17 +38,18 @@ def tile_macedensitytricksymmetriccontraction_x2_kernel(tc, h, w_words, w_scales
         banks = [ps.tile([P, 512], F32, name="bank%d" % i) for i in range(8)]
         t_bank, back_bank = banks[4], banks[5]
         ident = sb.tile([P, P], F32, name="ident", align_bytes=64)
-        coef_rows = sb.tile([P, C], BF16, name="coef_rows", align_bytes=64)
-        coef_f32 = sb.tile([P, C], F32, name="coef_f32", align_bytes=64)
-        coef_cols = sb.tile([P, 4, 8], F32, name="coef_cols", align_bytes=64)
+        coef_rows = sb.tile([P, P], BF16, name="coef_rows", align_bytes=64)
+        coef_f32 = sb.tile([P, P], F32, name="coef_f32", align_bytes=64)
+        coef_cols = sb.tile([P, 4 * J], F32, name="coef_cols", align_bytes=64)
         w_codes = sb.tile([P, 2, 2 * C], U8, name="w_codes", align_bytes=64)
         w_plane = sb.tile([P, 2, C], U8, name="w_plane", align_bytes=64)
         raw = ring("raw", RAW_SLOTS, [P, 4, 1024], BF16)
-        sorted_words = ring("sorted_words", 4, [P, 512], F32)
+        sorted_words = []
         stage = ring("stage", STAGE_SLOTS, [P, 2048], BF16)
         codes = ring("codes", CODE_SLOTS, [P, 512], U32)
         planes = ring("planes", CODE_SLOTS, [P, 512], U8)
         u_stage = ring("u_stage", 2, [P, 2, 2, 512], BF16)
+        u_rows = ring("u_rows", 2, [P, 4, C], BF16)
         u_codes = ring("u_codes", 2, [P, 512], U32)
         u_planes = ring("u_planes", 2, [P, 512], U8)
         squares = ring("squares", 2, [P, 3, 256], F32)
@@ -110,31 +111,37 @@ def tile_macedensitytricksymmetriccontraction_x2_kernel(tc, h, w_words, w_scales
             i = (n // 2) % CODE_SLOTS
             return codes[i][:, cols].bitcast(FP8X4), planes[i][:, cols]
 
-        def mix(g, j, bank, on_vector):
-            for t in range(4):
-                for gk in range(2):
-                    h_codes, h_plane = tile_operand(4 * g + t, gk)
-                    nc.tensor.matmul_mx(
-                        out=bank[:, P * t : P * (t + 1)],
-                        lhsT=h_codes,
-                        lhsT_scale=h_plane,
-                        rhs=w_codes[:, gk, 256 * j : 256 * (j + 1)].bitcast(FP4X4),
-                        rhs_scale=w_plane[:, gk, P * j : P * (j + 1)],
-                        start=(gk == 0),
-                        stop=(gk == 1),
-                    )
-            dst = u_stage[j // 2][:, g, j % 2, :].rearrange("p (c t) -> p c t", t=4)
-            src = bank[:].rearrange("p (t c) -> p c t", t=4)
+        def mix(g, t, bank, on_vector):
+            for gk in range(2):
+                h_codes, h_plane = tile_operand(4 * g + t, gk)
+                nc.tensor.matmul_mx(
+                    out=bank[:],
+                    lhsT=h_codes,
+                    lhsT_scale=h_plane,
+                    rhs=w_codes[:, gk, :].bitcast(FP4X4),
+                    rhs_scale=w_plane[:, gk, :],
+                    start=(gk == 0),
+                    stop=(gk == 1),
+                )
             if on_vector:
-                nc.vector.tensor_copy(out=dst, in_=src)
+                nc.vector.tensor_copy(out=u_rows[g][:, t, :], in_=bank[:])
             else:
-                nc.scalar.copy(out=dst, in_=src)
+                nc.scalar.copy(out=u_rows[g][:, t, :], in_=bank[:])
+
+        def group_u(g, jp):
+            dst = u_stage[jp][:, g, :, :].rearrange("p j (c t) -> p (j c) t", t=4)
+            nc.vector.tensor_copy(out=dst, in_=u_rows[g][:, :, 256 * jp : 256 * (jp + 1)].rearrange("p t c -> p c t"))
 
         def quantise_u(jp):
             nc.vector.quantize_mx(out=u_codes[jp][:].bitcast(FP8X4), scales=u_planes[jp][:], in_=u_stage[jp][:].rearrange("p g j c -> p (g j c)"))
 
         def cf(k, jj, row):
-            return coef_cols[:, unit(k)[jj][2], row : row + 1]
+            col = 4 * row + unit(k)[jj][2]
+            return coef_cols[:, col : col + 1]
+
+        def cf_psum(k, jj, row):
+            col = 256 + 4 * row + unit(k)[jj][2]
+            return t_bank[:, col : col + 1]
 
         def u_operand(j, gk, width):
             cols = slice(256 * gk + P * (j % 2), 256 * gk + P * (j % 2) + width)
@@ -161,11 +168,17 @@ def tile_macedensitytricksymmetriccontraction_x2_kernel(tc, h, w_words, w_scales
                 contract(pair[1][:, 256 + P * jj : 256 + P * (jj + 1)], lambda gk: u_operand(blocks[jj][2], gk, P), lambda gk: tile_operand(first[jj] + 3, gk))
             nc.scalar.activation(out=sq[:, 2, :], in_=pair[1][:, 0:256], func=ACT.Square, scale=math.sqrt(1.0 / 3.0))
 
+        def spans(k):
+            blocks = unit(k)
+            if blocks[0][2] == blocks[1][2]:
+                return [(0, slice(0, 256))]
+            return [(jj, slice(P * jj, P * (jj + 1))) for jj in range(2)]
+
         def affine_in_s(k):
-            for a, (slope, offset) in enumerate(((5, 4), (1, 0))):
-                for jj in range(2):
-                    s_cols = bank_pair(k)[1][:, 256 + P * jj : 256 + P * (jj + 1)]
-                    nc.scalar.activation(out=affine[k % 2][:, a, P * jj : P * (jj + 1)], in_=s_cols, func=ACT.Identity, scale=cf(k, jj, slope), bias=cf(k, jj, offset))
+            s_cols = bank_pair(k)[1][:, 256:512]
+            for a, (slope, offset) in ((1, (1, 0)), (0, (5, 4))):
+                for jj, cols in spans(k):
+                    nc.scalar.activation(out=affine[k % 2][:, a, cols], in_=s_cols[:, cols], func=ACT.Identity, scale=cf(k, jj, slope), bias=cf(k, jj, offset))
 
         def sum_squares(k):
             for jj in range(2):
@@ -181,17 +194,15 @@ def tile_macedensitytricksymmetriccontraction_x2_kernel(tc, h, w_words, w_scales
 
         def factors(k):
             for a, row in ((1, 3), (0, 6)):
-                for jj in range(2):
-                    cols = slice(P * jj, P * (jj + 1))
-                    nc.vector.scalar_tensor_tensor(out=qp[k % 2][:, a, cols], in0=t_bank[:, cols], scalar=cf(k, jj, row), in1=affine[k % 2][:, a, cols], op0=ALU.mult, op1=ALU.add)
+                for jj, cols in spans(k):
+                    nc.vector.scalar_tensor_tensor(out=qp[k % 2][:, a, cols], in0=t_bank[:, cols], scalar=cf_psum(k, jj, row), in1=affine[k % 2][:, a, cols], op0=ALU.mult, op1=ALU.add)
 
         def s_times_p(k):
             nc.vector.tensor_tensor(out=b0_t[k % 2][:], in0=bank_pair(k)[1][:, 256:512], in1=qp[k % 2][:, 1, :], op=ALU.mult)
 
         def finish_b0(k):
-            for jj in range(2):
-                cols = slice(P * jj, P * (jj + 1))
-                nc.vector.scalar_tensor_tensor(out=b0_t[k % 2][:, cols], in0=t_bank[:, cols], scalar=cf(k, jj, 2), in1=b0_t[k % 2][:, cols], op0=ALU.mult, op1=ALU.add)
+            for jj, cols in spans(k):
+                nc.vector.scalar_tensor_tensor(out=b0_t[k % 2][:, cols], in0=t_bank[:, cols], scalar=cf_psum(k, jj, 2), in1=b0_t[k % 2][:, cols], op0=ALU.mult, op1=ALU.add)
 
         def out_tile(k):
             (g, t, j), (g_last, t_last, j_last) = unit(k)
@@ -249,6 +260,20 @@ def tile_macedensitytricksymmetriccontraction_x2_kernel(tc, h, w_words, w_scales
             cols = slice(C * m + P * j, C * m + P * (j + 1))
             nc.vector.quantize_mx(out=o_codes[g][:, cols].bitcast(FP8X4), scales=o_planes[g][:, cols], in_=o_bf[:, slot, :])
 
+        def round_wide(m, jp, slot, eng):
+            dst = o_bf[:, slot : slot + 2, :].rearrange("p s (c t) -> p (s c) t", t=4)
+            src = o_f32[jp][:, m, :, :].rearrange("p t c -> p c t")
+            if eng == "vector":
+                nc.vector.tensor_copy(out=dst, in_=src)
+            elif eng == "scalar":
+                nc.scalar.copy(out=dst, in_=src)
+            else:
+                nc.gpsimd.tensor_scalar(out=dst, in0=src, scalar1=1.0, scalar2=0.0, op0=ALU.mult, op1=ALU.add)
+
+        def quantise_wide(m, jp, slot):
+            cols = slice(C * m + 256 * jp, C * m + 256 * (jp + 1))
+            nc.vector.quantize_mx(out=o_codes[0][:, cols].bitcast(FP8X4), scales=o_planes[0][:, cols], in_=o_bf[:, slot : slot + 2, :].rearrange("p s c -> p (s c)"))
+
         def store_words(g, first, last):
             dst = out_1[g].rearrange("p n t -> p (n t)").bitcast(I32).rearrange("p (m c) -> p m c", m=M)
             src = o_codes[g][:].bitcast(I32).rearrange("p (m c) -> p m c", m=M)
@@ -258,7 +283,7 @@ def tile_macedensitytricksymmetriccontraction_x2_kernel(tc, h, w_words, w_scales
             for quad in range(4):
                 (nc.scalar if g == 1 and quad % 2 else nc.sync).dma_start(out=out_2[g, 4 * quad : 4 * quad + 4, :].bitcast(I32), in_=o_planes[g][32 * quad : 32 * quad + 4, :].bitcast(I32))
 
-        nc.scalar.dma_start(out=coef_rows[0:J, :], in_=coef)
+        nc.scalar.dma_start(out=coef_rows[0 : 4 * J, :], in_=coef.rearrange("r (j c) -> (r j) c", j=4))
         nc.vector.memset(w_plane[:].rearrange("p g c -> p (g c)").bitcast(I32), 0)
         make_identity(nc, ident[:])
         nc.gpsimd.memset(coef_f32[:], 0.0)
@@ -277,87 +302,72 @@ def tile_macedensitytricksymmetriccontraction_x2_kernel(tc, h, w_words, w_scales
         load(2, slice(0, 2))
         for s in range(3, RAW_SLOTS):
             load(s, slice(0, 4))
-        nc.scalar.activation(out=coef_f32[0:J, :], in_=coef_rows[0:J, :], func=ACT.Identity)
+        nc.scalar.activation(out=coef_f32[0 : 4 * J, :], in_=coef_rows[0 : 4 * J, :], func=ACT.Identity)
+
+        def head_turn(n, bank):
+            sort_words(n + 2)
+            turn_in(n, banks[bank], n in VCOPY)
+            if n % 4 == 3 and RAW_SLOTS + n // 4 < 10:
+                load(RAW_SLOTS + n // 4, slice(0, 4))
 
         sort_words(0)
         sort_words(1)
         for n in range(6):
-            sort_words(n + 2)
-            turn_in(n, banks[4 + n % 4], n in VCOPY)
+            head_turn(n, 4 + n % 4)
             if n in (2, 4):
                 quantise_in(n // 2 - 1)
-            if n == 3:
-                load(RAW_SLOTS, slice(0, 4))
         mix(0, 0, banks[0], False)
-        mix(0, 1, banks[1], False)
+        mix(0, 1, banks[1], True)
         quantise_in(2)
-        turn_in(6, banks[6], 6 in VCOPY)
-        turn_in(7, banks[7], 7 in VCOPY)
-        load(RAW_SLOTS + 1, slice(0, 4))
-        sort_words(8)
-        sort_words(9)
+        head_turn(6, 6)
+        head_turn(7, 7)
         mix(0, 2, banks[2], False)
+        mix(0, 3, banks[3], False)
         quantise_in(3)
-        mix(0, 3, banks[3], True)
-        turn_in(8, banks[4], 8 in VCOPY)
-        turn_in(9, banks[5], 9 in VCOPY)
-        sort_words(10)
-        sort_words(11)
-        mix(1, 0, banks[6], False)
-        mix(1, 1, banks[7], False)
-        quantise_in(4)
-        turn_in(10, banks[0], 10 in VCOPY)
-        turn_in(11, banks[1], 11 in VCOPY)
-        load(RAW_SLOTS + 2, slice(0, 4))
-        quantise_u(0)
-        for j in range(4):
-            nc.tensor.transpose(banks[4][:, P * j : P * (j + 1)], coef_f32[:, P * j : P * (j + 1)], ident[:])
-        nc.vector.tensor_copy(out=coef_cols[:], in_=banks[4][:].rearrange("p (j r) -> p j r", j=4)[:, :, 0:8])
-        sort_words(12)
-        sort_words(13)
+        head_turn(8, 4)
+        head_turn(9, 5)
+        group_u(0, 0)
+        mix(1, 0, banks[0], False)
+        mix(1, 1, banks[1], True)
         mix(1, 2, banks[2], False)
+        mix(1, 3, banks[3], True)
+        quantise_in(4)
+        head_turn(10, 6)
+        head_turn(11, 7)
+        group_u(1, 0)
+        nc.tensor.transpose(t_bank[:, 256 : 256 + P], coef_f32[:], ident[:])
+        nc.scalar.copy(out=coef_cols[:], in_=t_bank[:, 256 : 256 + 4 * J])
         quantise_in(5)
-        sort_words(14)
-        sort_words(15)
-        mix(1, 3, banks[3], False)
-        turn_in(12, banks[5], 12 in VCOPY)
-        turn_in(13, banks[6], 13 in VCOPY)
+        quantise_u(0)
+        head_turn(12, 5)
+        head_turn(13, 2)
+        head_turn(14, 3)
+        head_turn(15, 6)
         project(0)
-        quantise_u(1)
-        sort_words(16)
-        sort_words(17)
-        turn_in(14, banks[7], 14 in VCOPY)
-        turn_in(15, banks[5], 15 in VCOPY)
-        load(RAW_SLOTS + 3, slice(0, 4))
+        group_u(0, 1)
+        group_u(1, 1)
         quantise_in(6)
-        sort_words(18)
-        sort_words(19)
+        quantise_u(1)
+        head_turn(16, 7)
+        head_turn(17, 5)
         affine_in_s(0)
-        turn_in(16, banks[6], 16 in VCOPY)
         sum_squares(0)
         quantise_in(7)
         factors(0)
         s_times_p(0)
-        turn_in(17, banks[7], 17 in VCOPY)
-        turn_in(18, banks[5], 18 in VCOPY)
-        turn_in(19, banks[6], 19 in VCOPY)
-        sort_words(20)
-        finish_b0(0)
+        head_turn(18, 6)
+        head_turn(19, 7)
         quantise_in(8)
+        finish_b0(0)
         quantise_in(9)
 
         plan = {
-            7: [(0, 2, "g", 0)],
-            8: [(4, 2, "g", 0)],
-            9: [(2, 2, "g", 0)],
-            10: [(6, 2, "g", 0)],
-            11: [(10, 1, "scalar", 10), (11, 1, "vector", 8), (8, 2, "g", 0)],
-            12: [(12, 2, "g", 0)],
-            13: [(16, 1, "scalar", 6), (17, 1, "vector", 4), (14, 2, "g", 0)],
+            13: [(17, 1, "vector", 4), (16, 1, "scalar", 6)],
             14: [(20, 1, "scalar", 10), (21, 1, "vector", 8), (18, 2, "g", 0)],
             15: [(24, 1, "scalar", 6), (25, 1, "vector", 4), (22, 2, "g", 0)],
         }
 
+        wide = {7: (2, 0), 8: (3, 0), 9: (1, 0), 10: (0, 0), 11: (2, 1), 12: (3, 1), 13: (1, 1)}
         for k in range(1, UNITS):
             tiles = [18 + 2 * k, 19 + 2 * k] if k <= 10 else []
             mine = plan.get(k, [])
@@ -371,6 +381,8 @@ def tile_macedensitytricksymmetriccontraction_x2_kernel(tc, h, w_words, w_scales
             for n, count, eng, slot in mine:
                 if eng == "g":
                     round_out(n, count, slot, G_ENG)
+            if k in wide:
+                round_wide(*wide[k], 0, G_ENG)
             if tiles:
                 turn_in(tiles[0], banks[7 - k % 2], False)
             sum_squares(k)
@@ -390,6 +402,8 @@ def tile_macedensitytricksymmetriccontraction_x2_kernel(tc, h, w_words, w_scales
             for n, count, eng, slot in mine:
                 if eng != "g":
                     round_out(n, count, slot, eng)
+            if k == 11:
+                round_wide(0, 1, 8, "vector")
             if tiles:
                 quantise_in(tiles[0] // 2)
             if k == UNITS - 1:
@@ -397,6 +411,10 @@ def tile_macedensitytricksymmetriccontraction_x2_kernel(tc, h, w_words, w_scales
             for n, count, eng, slot in mine:
                 for i in range(count):
                     quantise_out(n + i, slot + i)
+            if k == 12:
+                quantise_wide(0, 1, 8)
+            if k in wide:
+                quantise_wide(*wide[k], 0)
             if k == 10:
                 store_words(0, 0, 2)
             if k == 13:

import math
from contextlib import ExitStack

import concourse.mybir as mybir
from concourse.masks import make_identity

F32 = mybir.dt.float32
BF16 = mybir.dt.bfloat16
I32 = mybir.dt.int32
U32 = mybir.dt.uint32
U8 = mybir.dt.uint8
FP8X4 = mybir.dt.float8_e4m3fn_x4
FP4X4 = mybir.dt.float4_e2m1fn_x4
ACT = mybir.ActivationFunctionType
ALU = mybir.AluOpType

P = 128
R, N, D, C, M, J = 1024, 1024, 1024, 512, 4, 7
FLOPS = 2 * N * D * C + 2 * M * R * N * C
UNITS = 16
SORTED = ()
VCOPY = (1, 3, 7, 11, 15, 19, 21, 23, 25, 27, 29, 31, 33, 37)
G_ENG = "gpsimd"
M_ORDER = (2, 3, 1, 0)
RAW_SLOTS, STAGE_SLOTS, CODE_SLOTS, OUT_SLOTS, OBF_SLOTS = 6, 3, 12, 4, 12


def tile_macedensitytricksymmetriccontraction_x2_kernel(tc, h, w_words, w_scales, e, coef, out_0, out_1, out_2):
    nc = tc.nc
    with ExitStack() as ctx:
        sb = ctx.enter_context(tc.tile_pool(name="sb", bufs=1))
        ps = ctx.enter_context(tc.psum_pool(name="ps", bufs=1))
        ctx.enter_context(tc.manual_schedule())

        def ring(name, count, shape, dtype):
            return [sb.tile(shape, dtype, name="%s%d" % (name, i), align_bytes=64) for i in range(count)]

        banks = [ps.tile([P, 512], F32, name="bank%d" % i) for i in range(8)]
        t_bank, back_bank = banks[4], banks[5]
        ident = sb.tile([P, P], F32, name="ident", align_bytes=64)
        coef_rows = sb.tile([P, P], BF16, name="coef_rows", align_bytes=64)
        coef_f32 = sb.tile([P, P], F32, name="coef_f32", align_bytes=64)
        coef_cols = sb.tile([P, 4 * J], F32, name="coef_cols", align_bytes=64)
        w_codes = sb.tile([P, 2, 2 * C], U8, name="w_codes", align_bytes=64)
        w_plane = sb.tile([P, 2, C], U8, name="w_plane", align_bytes=64)
        raw = ring("raw", RAW_SLOTS, [P, 4, 1024], BF16)
        sorted_words = []
        stage = ring("stage", STAGE_SLOTS, [P, 2048], BF16)
        codes = ring("codes", CODE_SLOTS, [P, 512], U32)
        planes = ring("planes", CODE_SLOTS, [P, 512], U8)
        u_stage = ring("u_stage", 2, [P, 2, 2, 512], BF16)
        u_rows = ring("u_rows", 2, [P, 4, C], BF16)
        u_codes = ring("u_codes", 2, [P, 512], U32)
        u_planes = ring("u_planes", 2, [P, 512], U8)
        squares = ring("squares", 2, [P, 3, 256], F32)
        affine = ring("affine", 2, [P, 2, 256], F32)
        qp = ring("qp", 2, [P, 2, 256], F32)
        b0_t = ring("b0_t", 2, [P, 256], F32)
        q_rows = ring("q_rows", 2, [P, 256], F32)
        o_f32 = ring("o_f32", OUT_SLOTS, [P, M, 4, 256], F32)
        o_bf = sb.tile([P, OBF_SLOTS, 512], BF16, name="o_bf", align_bytes=64)
        o_codes = ring("o_codes", 2, [P, M * C], U32)
        o_planes = ring("o_planes", 2, [P, M * C], U8)

        def unit(k):
            if k < 12:
                return [(k // 8, (k // 2) % 4, 2 * (k % 2) + jj) for jj in range(2)]
            return [(1, t, k - 12) for t in (2, 3)]

        def bank_pair(k):
            first = 2 * (k % 2) if k < 12 else (6, 0, 2, 6)[k - 12]
            return banks[first : first + 2]

        def load(s, part):
            if s < 2:
                src = h[512 * s : 512 * (s + 1), :].rearrange("(p t) k -> p t k", t=4)[:, part, :]
                nc.sync.dma_start(out=raw[s][:, part, :], in_=src)
            else:
                g, t = (s - 2) // 4, (s - 2) % 4
                src = e[:, 512 * g : 512 * (g + 1), :].rearrange("m (p t) k -> p t m k", t=4)[:, t, part, :]
                nc.sync.dma_start(out=raw[s % RAW_SLOTS][:, part, :], in_=src)

        def sort_words(n):
            if n in SORTED:
                s, a = n // 4, n % 4
                words = raw[s % RAW_SLOTS][:, a if s < 2 else M_ORDER[a], :].bitcast(F32)
                nc.vector.tensor_copy(out=sorted_words[n % 4][:].rearrange("p (g u r) -> p g u r", g=2, u=2), in_=words.rearrange("p (g r u) -> p g u r", g=2, u=2))

        def turn_in(n, bank, on_vector):
            s, a = n // 4, n % 4
            words = raw[s % RAW_SLOTS][:, a if s < 2 else M_ORDER[a], :].bitcast(F32)
            for gk in range(2):
                for u in range(2):
                    col = (2 * gk + u) * P
                    if n in SORTED:
                        nc.tensor.transpose(bank[:, col : col + P], sorted_words[n % 4][:, col : col + P], ident[:])
                    else:
                        nc.tensor.transpose(bank[:, col : col + P], words[:, 256 * gk + u : 256 * (gk + 1) : 2], ident[:])
            dst = stage[(n // 2) % STAGE_SLOTS][:, 1024 * (n % 2) : 1024 * (n % 2 + 1)].bitcast(F32).rearrange("p (g r u) -> p g r u", g=2, u=2)
            src = bank[:].rearrange("p (g u r) -> p g r u", g=2, u=2)
            if on_vector:
                nc.vector.tensor_copy(out=dst, in_=src)
            else:
                nc.scalar.copy(out=dst, in_=src)

        def quantise_in(i):
            nc.vector.quantize_mx(out=codes[i % CODE_SLOTS][:].bitcast(FP8X4), scales=planes[i % CODE_SLOTS][:], in_=stage[i % STAGE_SLOTS][:])

        def tile_operand(n, gk):
            cols = slice(256 * (n % 2) + P * gk, 256 * (n % 2) + P * (gk + 1))
            i = (n // 2) % CODE_SLOTS
            return codes[i][:, cols].bitcast(FP8X4), planes[i][:, cols]

        def mix(g, t, bank, on_vector):
            for gk in range(2):
                h_codes, h_plane = tile_operand(4 * g + t, gk)
                nc.tensor.matmul_mx(
                    out=bank[:],
                    lhsT=h_codes,
                    lhsT_scale=h_plane,
                    rhs=w_codes[:, gk, :].bitcast(FP4X4),
                    rhs_scale=w_plane[:, gk, :],
                    start=(gk == 0),
                    stop=(gk == 1),
                )
            if on_vector:
                nc.vector.tensor_copy(out=u_rows[g][:, t, :], in_=bank[:])
            else:
                nc.scalar.copy(out=u_rows[g][:, t, :], in_=bank[:])

        def group_u(g, jp):
            dst = u_stage[jp][:, g, :, :].rearrange("p j (c t) -> p (j c) t", t=4)
            nc.vector.tensor_copy(out=dst, in_=u_rows[g][:, :, 256 * jp : 256 * (jp + 1)].rearrange("p t c -> p c t"))

        def quantise_u(jp):
            nc.vector.quantize_mx(out=u_codes[jp][:].bitcast(FP8X4), scales=u_planes[jp][:], in_=u_stage[jp][:].rearrange("p g j c -> p (g j c)"))

        def cf(k, jj, row):
            col = 4 * row + unit(k)[jj][2]
            return coef_cols[:, col : col + 1]

        def cf_psum(k, jj, row):
            col = 256 + 4 * row + unit(k)[jj][2]
            return t_bank[:, col : col + 1]

        def u_operand(j, gk, width):
            cols = slice(256 * gk + P * (j % 2), 256 * gk + P * (j % 2) + width)
            return u_codes[j // 2][:, cols].bitcast(FP8X4), u_planes[j // 2][:, cols]

        def contract(out, stationary, moving):
            for gk in range(2):
                (l_codes, l_plane), (r_codes, r_plane) = stationary(gk), moving(gk)
                nc.tensor.matmul_mx(out=out, lhsT=l_codes, lhsT_scale=l_plane, rhs=r_codes, rhs_scale=r_plane, start=(gk == 0), stop=(gk == 1))

        def project(k):
            blocks = unit(k)
            first = [8 + 4 * (4 * g + t) for g, t, j in blocks]
            pair = bank_pair(k)
            sq = squares[k % 2]
            width = 256 if first[0] == first[1] else P
            for a in range(3):
                for jj in range(256 // width):
                    col = 256 * (a % 2) + P * jj
                    contract(pair[a // 2][:, col : col + width], lambda gk: tile_operand(first[jj] + a, gk), lambda gk: u_operand(blocks[jj][2], gk, width))
                if a == 1:
                    nc.scalar.activation(out=sq[:, 0:2, :].rearrange("p a c -> p (a c)"), in_=pair[0][:], func=ACT.Square, scale=math.sqrt(1.0 / 3.0))
            for jj in range(2):
                contract(pair[1][:, 256 + P * jj : 256 + P * (jj + 1)], lambda gk: u_operand(blocks[jj][2], gk, P), lambda gk: tile_operand(first[jj] + 3, gk))
            nc.scalar.activation(out=sq[:, 2, :], in_=pair[1][:, 0:256], func=ACT.Square, scale=math.sqrt(1.0 / 3.0))

        def spans(k):
            blocks = unit(k)
            if blocks[0][2] == blocks[1][2]:
                return [(0, slice(0, 256))]
            return [(jj, slice(P * jj, P * (jj + 1))) for jj in range(2)]

        def affine_in_s(k):
            s_cols = bank_pair(k)[1][:, 256:512]
            for a, (slope, offset) in ((1, (1, 0)), (0, (5, 4))):
                for jj, cols in spans(k):
                    nc.scalar.activation(out=affine[k % 2][:, a, cols], in_=s_cols[:, cols], func=ACT.Identity, scale=cf(k, jj, slope), bias=cf(k, jj, offset))

        def sum_squares(k):
            for jj in range(2):
                for a in range(3):
                    nc.tensor.matmul(
                        out=t_bank[:, P * jj : P * (jj + 1)],
                        lhsT=squares[k % 2][:, a, P * jj : P * (jj + 1)],
                        rhs=ident[:],
                        start=(a == 0),
                        stop=(a == 2),
                        is_transpose=True,
                    )

        def factors(k):
            for a, row in ((1, 3), (0, 6)):
                for jj, cols in spans(k):
                    nc.vector.scalar_tensor_tensor(out=qp[k % 2][:, a, cols], in0=t_bank[:, cols], scalar=cf_psum(k, jj, row), in1=affine[k % 2][:, a, cols], op0=ALU.mult, op1=ALU.add)

        def s_times_p(k):
            nc.vector.tensor_tensor(out=b0_t[k % 2][:], in0=bank_pair(k)[1][:, 256:512], in1=qp[k % 2][:, 1, :], op=ALU.mult)

        def finish_b0(k):
            for jj, cols in spans(k):
                nc.vector.scalar_tensor_tensor(out=b0_t[k % 2][:, cols], in0=t_bank[:, cols], scalar=cf_psum(k, jj, 2), in1=b0_t[k % 2][:, cols], op0=ALU.mult, op1=ALU.add)

        def out_tile(k):
            (g, t, j), (g_last, t_last, j_last) = unit(k)
            o = o_f32[2 * g + j // 2]
            if t == t_last:
                return o[:, :, t, :].rearrange("p m (b c) -> p m b c", b=2)
            return o[:, :, t : t + 2, P * (j % 2) : P * (j % 2 + 1)]

        def turn_back(side, src):
            for jj in range(2):
                col = 256 * side + P * jj
                nc.tensor.transpose(back_bank[:, col : col + P], src[:, P * jj : P * (jj + 1)], ident[:])

        def copy_q(k):
            nc.scalar.copy(out=q_rows[k % 2][:], in_=back_bank[:, 0:256])

        def copy_b0(k):
            nc.scalar.copy(out=out_tile(k)[:, 0, :, :], in_=back_bank[:, 256:512].rearrange("p (b c) -> p b c", b=2))

        def products(k, half):
            bank, o, q = bank_pair(k)[half], out_tile(k), q_rows[k % 2]
            if half == 0:
                nc.vector.tensor_tensor(
                    out=o[:, 2:4, :, :],
                    in0=bank[:].rearrange("p (a b c) -> p a b c", a=2, b=2),
                    in1=q[:].rearrange("p (a b c) -> p a b c", a=1, b=2).to_broadcast([P, 2, 2, P]),
                    op=ALU.mult,
                )
            else:
                nc.vector.tensor_tensor(out=o[:, 1, :, :], in0=bank[:, 0:256].rearrange("p (b c) -> p b c", b=2), in1=q[:].rearrange("p (b c) -> p b c", b=2), op=ALU.mult)

        def store_rows(k, m_first, m_last):
            (g, t, j), (g_last, t_last, j_last) = unit(k)
            rows = out_0[:, 512 * g : 512 * (g + 1), P * j : P * (j_last + 1)].rearrange("m (p t) c -> p m t c", t=4)
            o = o_f32[2 * g + j // 2][:, :, :, P * (j % 2) : P * (j_last % 2 + 1)]
            if m_last - m_first == 1:
                nc.sync.dma_start(out=rows[:, m_first, t : t_last + 1, :], in_=o[:, m_first, t : t_last + 1, :])
            else:
                for tt in range(t, t_last + 1):
                    nc.sync.dma_start(out=rows[:, m_first:m_last, tt, :], in_=o[:, m_first:m_last, tt, :])

        def round_out(n, count, slot, eng):
            g, j, m = n // 16, (n // 4) % 4, (n + 2) % 4
            dst = o_bf[:, slot : slot + count, :].rearrange("p m (c t) -> p m c t", t=4)
            src = o_f32[2 * g + j // 2][:, m : m + count, :, P * (j % 2) : P * (j % 2 + 1)].rearrange("p m t c -> p m c t")
            if eng == "vector":
                nc.vector.tensor_copy(out=dst, in_=src)
            elif eng == "scalar":
                nc.scalar.copy(out=dst, in_=src)
            else:
                nc.gpsimd.tensor_scalar(out=dst, in0=src, scalar1=1.0, scalar2=0.0, op0=ALU.mult, op1=ALU.add)

        def quantise_out(n, slot):
            g, j, m = n // 16, (n // 4) % 4, (n + 2) % 4
            cols = slice(C * m + P * j, C * m + P * (j + 1))
            nc.vector.quantize_mx(out=o_codes[g][:, cols].bitcast(FP8X4), scales=o_planes[g][:, cols], in_=o_bf[:, slot, :])

        def round_wide(m, jp, slot, eng):
            dst = o_bf[:, slot : slot + 2, :].rearrange("p s (c t) -> p (s c) t", t=4)
            src = o_f32[jp][:, m, :, :].rearrange("p t c -> p c t")
            if eng == "vector":
                nc.vector.tensor_copy(out=dst, in_=src)
            elif eng == "scalar":
                nc.scalar.copy(out=dst, in_=src)
            else:
                nc.gpsimd.tensor_scalar(out=dst, in0=src, scalar1=1.0, scalar2=0.0, op0=ALU.mult, op1=ALU.add)

        def quantise_wide(m, jp, slot):
            cols = slice(C * m + 256 * jp, C * m + 256 * (jp + 1))
            nc.vector.quantize_mx(out=o_codes[0][:, cols].bitcast(FP8X4), scales=o_planes[0][:, cols], in_=o_bf[:, slot : slot + 2, :].rearrange("p s c -> p (s c)"))

        def store_words(g, first, last):
            dst = out_1[g].rearrange("p n t -> p (n t)").bitcast(I32).rearrange("p (m c) -> p m c", m=M)
            src = o_codes[g][:].bitcast(I32).rearrange("p (m c) -> p m c", m=M)
            nc.sync.dma_start(out=dst[:, :, P * first : P * last], in_=src[:, :, P * first : P * last])

        def store_scales(g):
            for quad in range(4):
                (nc.scalar if g == 1 and quad % 2 else nc.sync).dma_start(out=out_2[g, 4 * quad : 4 * quad + 4, :].bitcast(I32), in_=o_planes[g][32 * quad : 32 * quad + 4, :].bitcast(I32))

        nc.scalar.dma_start(out=coef_rows[0 : 4 * J, :], in_=coef.rearrange("r (j c) -> (r j) c", j=4))
        nc.vector.memset(w_plane[:].rearrange("p g c -> p (g c)").bitcast(I32), 0)
        make_identity(nc, ident[:])
        nc.gpsimd.memset(coef_f32[:], 0.0)
        load(0, slice(0, 1))
        load(0, slice(1, 2))
        load(0, slice(2, 4))
        for quad in range(4):
            nc.scalar.dma_start(
                out=w_plane[32 * quad : 32 * quad + 4, :, :].bitcast(I32),
                in_=w_scales[:, 4 * quad : 4 * quad + 4, :].rearrange("g r c -> r g c").bitcast(I32),
            )
        load(1, slice(0, 2))
        nc.sync.dma_start(out=w_codes[:].bitcast(I32), in_=w_words.rearrange("g p n -> p g n").bitcast(I32))
        load(1, slice(2, 4))
        load(2, slice(2, 4))
        load(2, slice(0, 2))
        for s in range(3, RAW_SLOTS):
            load(s, slice(0, 4))
        nc.scalar.activation(out=coef_f32[0 : 4 * J, :], in_=coef_rows[0 : 4 * J, :], func=ACT.Identity)

        def head_turn(n, bank):
            sort_words(n + 2)
            turn_in(n, banks[bank], n in VCOPY)
            if n % 4 == 3 and RAW_SLOTS + n // 4 < 10:
                load(RAW_SLOTS + n // 4, slice(0, 4))

        sort_words(0)
        sort_words(1)
        for n in range(6):
            head_turn(n, 4 + n % 4)
            if n in (2, 4):
                quantise_in(n // 2 - 1)
        mix(0, 0, banks[0], False)
        mix(0, 1, banks[1], True)
        quantise_in(2)
        head_turn(6, 6)
        head_turn(7, 7)
        mix(0, 2, banks[2], False)
        mix(0, 3, banks[3], False)
        quantise_in(3)
        head_turn(8, 4)
        head_turn(9, 5)
        group_u(0, 0)
        mix(1, 0, banks[0], False)
        mix(1, 1, banks[1], True)
        mix(1, 2, banks[2], False)
        mix(1, 3, banks[3], True)
        quantise_in(4)
        head_turn(10, 6)
        head_turn(11, 7)
        group_u(1, 0)
        nc.tensor.transpose(t_bank[:, 256 : 256 + P], coef_f32[:], ident[:])
        nc.scalar.copy(out=coef_cols[:], in_=t_bank[:, 256 : 256 + 4 * J])
        quantise_in(5)
        quantise_u(0)
        head_turn(12, 5)
        head_turn(13, 2)
        head_turn(14, 3)
        head_turn(15, 6)
        project(0)
        group_u(0, 1)
        group_u(1, 1)
        quantise_in(6)
        quantise_u(1)
        head_turn(16, 7)
        head_turn(17, 5)
        affine_in_s(0)
        sum_squares(0)
        quantise_in(7)
        factors(0)
        s_times_p(0)
        head_turn(18, 6)
        head_turn(19, 7)
        quantise_in(8)
        finish_b0(0)
        quantise_in(9)

        plan = {
            13: [(17, 1, "vector", 4), (16, 1, "scalar", 6)],
            14: [(20, 1, "scalar", 10), (21, 1, "vector", 8), (18, 2, "g", 0)],
            15: [(24, 1, "scalar", 6), (25, 1, "vector", 4), (22, 2, "g", 0)],
        }

        wide = {7: (2, 0), 8: (3, 0), 9: (1, 0), 10: (0, 0), 11: (2, 1), 12: (3, 1), 13: (1, 1)}
        for k in range(1, UNITS):
            tiles = [18 + 2 * k, 19 + 2 * k] if k <= 10 else []
            mine = plan.get(k, [])
            project(k)
            turn_back(0, qp[(k - 1) % 2][:, 0, :])
            copy_q(k - 1)
            products(k - 1, 0)
            if k < 12:
                products(k - 1, 1)
            affine_in_s(k)
            for n, count, eng, slot in mine:
                if eng == "g":
                    round_out(n, count, slot, G_ENG)
            if k in wide:
                round_wide(*wide[k], 0, G_ENG)
            if tiles:
                turn_in(tiles[0], banks[7 - k % 2], False)
            sum_squares(k)
            turn_back(1, b0_t[(k - 1) % 2][:])
            copy_b0(k - 1)
            factors(k)
            s_times_p(k)
            if k >= 12:
                products(k - 1, 1)
            store_rows(k - 1, 0, 4)
            if tiles:
                turn_in(tiles[1], banks[6 + k % 2], tiles[1] in VCOPY)
                sort_words(tiles[0] + 2)
            finish_b0(k)
            if tiles:
                sort_words(tiles[1] + 2)
            for n, count, eng, slot in mine:
                if eng != "g":
                    round_out(n, count, slot, eng)
            if k == 11:
                round_wide(0, 1, 8, "vector")
            if tiles:
                quantise_in(tiles[0] // 2)
            if k == UNITS - 1:
                break
            for n, count, eng, slot in mine:
                for i in range(count):
                    quantise_out(n + i, slot + i)
            if k == 12:
                quantise_wide(0, 1, 8)
            if k in wide:
                quantise_wide(*wide[k], 0)
            if k == 10:
                store_words(0, 0, 2)
            if k == 13:
                store_words(0, 2, 4)
                store_scales(0)
            if k >= 14:
                store_words(1, k - 14, k - 13)

        last = UNITS - 1
        turn_back(0, qp[last % 2][:, 0, :])
        copy_q(last)
        turn_back(1, b0_t[last % 2][:])
        round_out(26, 1, 2, "scalar")
        products(last, 0)
        products(last, 1)
        store_rows(last, 1, 4)
        copy_b0(last)
        store_rows(last, 0, 1)
        round_out(27, 1, 3, "scalar")
        round_out(28, 1, 8, "scalar")
        round_out(30, 1, 10, "scalar")
        for n, count, eng, slot in plan[last]:
            for i in range(count):
                quantise_out(n + i, slot + i)
        store_words(1, 1, 2)
        round_out(29, 1, 9, "vector")
        round_out(31, 1, 11, "vector")
        quantise_out(26, 2)
        quantise_out(27, 3)
        store_words(1, 2, 3)
        for n, slot in ((29, 9), (31, 11), (28, 8), (30, 10)):
            quantise_out(n, slot)
        store_words(1, 3, 4)
        store_scales(1)
